import numpy as np
import ml_dtypes


def mxq(x, axis, fmt="e4m3"):
    dtype, down = {"e4m3": (ml_dtypes.float8_e4m3fn, 7), "e5m2": (ml_dtypes.float8_e5m2, 14)}[fmt]
    v = np.moveaxis(np.asarray(x, np.float32).astype(ml_dtypes.bfloat16).astype(np.float64), axis, -1)
    blocks = v.reshape(v.shape[:-1] + (-1, 32))
    amax = np.abs(blocks).max(-1, keepdims=True)
    byte = np.maximum(np.where(amax > 0, np.frexp(amax)[1] - 1 + 127, 0) - down, 1)
    scale = np.exp2(byte - 127.0)
    codes = (blocks / scale).astype(np.float32).astype(dtype).astype(np.float64)
    return np.moveaxis((codes * scale).reshape(v.shape), -1, axis)


WIDE = False


def mx_kscale(k):
    if not WIDE:
        return np.ones(k)
    levels = np.array([10, -10, 5, -5, 0])
    if k % 512:
        return np.exp2(np.random.permutation(np.resize(levels, k // 32))).repeat(32)
    a = np.empty((k // 512, 16))
    for p in range(k // 512):
        a[p, :8] = np.random.permutation(np.resize(levels, 8))
        for g in range(8):
            far = levels[np.abs(levels - a[p, g]) >= 10]
            a[p, g + 8] = far[np.random.randint(len(far))]
    return np.exp2(a.ravel()).repeat(32)


def f64(x):
    return np.asarray(x).astype(np.float64)


E2M1 = np.array([0.0, 0.5, 1.0, 1.5, 2.0, 3.0, 4.0, 6.0, -0.0, -0.5, -1.0, -1.5, -2.0, -3.0, -4.0, -6.0])


def pack_weight(w, fmt):
    k, n = w.shape
    w = f64(np.asarray(w, np.float32).astype(ml_dtypes.bfloat16)).reshape(k // 32, 32, n)
    amax = np.abs(w).max(1)
    if fmt == "e4m3":
        byte = np.frexp(amax)[1] - 1 + 127 - 7
    else:
        mant, ex = np.frexp(amax / 6.0)
        byte = np.where(mant > 0.5, ex, ex - 1) + 127
    byte = np.clip(np.where(amax > 0, byte, 1), 1, 254)
    scaled = (w * np.exp2(127.0 - byte)[:, None, :]).reshape(k, n).astype(np.float32)
    by_word = np.ascontiguousarray(scaled.reshape(k // 512, 128, 4, n).transpose(0, 1, 3, 2))
    if fmt == "e4m3":
        words = by_word.astype(ml_dtypes.float8_e4m3fn).view(np.uint8)
    else:
        c = by_word.astype(ml_dtypes.float4_e2m1fn).view(np.uint8) & 0xF
        words = (c[..., 0::2] | (c[..., 1::2] << 4)).reshape(k // 512, 128, 2 * n)
    return np.ascontiguousarray(words), np.ascontiguousarray(byte.astype(np.uint8).reshape(k // 512, 16, n))


def unpack_weight(words, scales, fmt):
    g, _, n = scales.shape
    words = np.ascontiguousarray(words).reshape(g, 128, n, -1)
    if fmt == "e4m3":
        vals = words.view(ml_dtypes.float8_e4m3fn).astype(np.float64)
    else:
        nib = np.empty((g, 128, n, 4), np.uint8)
        nib[..., 0::2] = words & 0xF
        nib[..., 1::2] = words >> 4
        vals = E2M1[nib]
    vals = vals * np.repeat(np.exp2(scales.astype(np.float64) - 127.0), 8, axis=1)[..., None]
    return vals.transpose(0, 1, 3, 2).reshape(g * 512, n)


def gelu(v):
    return 0.5 * v * (1.0 + np.tanh(np.sqrt(2.0 / np.pi) * (v + 0.044715 * v**3)))


O, K, M, T = 512, 3072, 1024, 512


def setup_inputs():
    n = np.random.standard_normal
    s = mx_kscale(K)[:, None]
    x = n((K, T)); x[:O] *= 6.0
    w = n((K, M)) / np.sqrt(K) / s; w[:O] /= 2.0
    p_w8 = pack_weight(w[:O], "e4m3")
    p_w4 = pack_weight(w[O:], "e2m1")
    return {
        "x": (x * s).astype(np.float32),
        "w8_words": p_w8[0],
        "w8_scales": p_w8[1],
        "w4_words": p_w4[0],
        "w4_scales": p_w4[1],
        "b": (0.3 * n(1024)).astype(np.float32),
    }


def reference(x, w8_words, w8_scales, w4_words, w4_scales, b):
    x_ = mxq(f64(x), 0, "e4m3")
    w8_ = unpack_weight(w8_words, w8_scales, "e4m3")
    w4_ = unpack_weight(w4_words, w4_scales, "e2m1")
    y = w8_.T @ x_[:O] + w4_.T @ x_[O:]
    return gelu(y + f64(b)[:, None])

from contextlib import ExitStack

import concourse.mybir as mybir
from concourse.masks import make_identity

O, K, M, T = 512, 3072, 1024, 512
FLOPS = 2 * K * M * T

F32 = mybir.dt.float32
BF16 = mybir.dt.bfloat16
I32 = mybir.dt.int32
U32 = mybir.dt.uint32
U8 = mybir.dt.uint8
FP8X4 = mybir.dt.float8_e4m3fn_x4
FP4X4 = mybir.dt.float4_e2m1fn_x4
GELU = mybir.ActivationFunctionType.Gelu_apprx_tanh

P = 128
PACK = 4
K_PASS = P * PACK
N_K = K // K_PASS
N_M = M // P
HALF = T // 2
V_COLS = 176


def tile_mix_outl_fm_gelu_kernel(tc, x, w8_words, w8_scales, w4_words, w4_scales, b, out):
    nc = tc.nc
    with ExitStack() as ctx:
        keep = ctx.enter_context(tc.tile_pool(name="keep", bufs=1))
        psum = ctx.enter_context(tc.psum_pool(name="psum", bufs=1))

        raw = [keep.tile([P, PACK, T], F32, name="raw%d" % k, align_bytes=64) for k in range(N_K)]
        grouped = [keep.tile([P, T, PACK], BF16, name="grouped%d" % k, align_bytes=64) for k in range(N_K)]
        codes = [keep.tile([P, T], U32, name="codes%d" % k, align_bytes=64) for k in range(N_K)]
        xscales = [keep.tile([P, T], U8, name="xscales%d" % k, align_bytes=64) for k in range(N_K)]
        w8 = keep.tile([P, M], U32, name="w8", align_bytes=64)
        w4 = [keep.tile([P, 2 * M], U8, name="w4_%d" % a, align_bytes=64) for a in range(N_K - 1)]
        s8 = keep.tile([P, M], U8, name="s8", align_bytes=64)
        s4 = keep.tile([P, (N_K - 1) * M], U8, name="s4", align_bytes=64)
        result = [keep.tile([P, T], F32, name="result%d" % m) for m in range(N_M)]
        b_rows = keep.tile([P, P], F32, name="b_rows")
        b_cols = keep.tile([P, N_M], F32, name="b_cols")
        ident = keep.tile([P, P], F32, name="ident")
        warm = keep.tile([P, 1], F32, name="warm")

        def load_x(k, h=None):
            src = x[k * K_PASS : (k + 1) * K_PASS, :].rearrange("(p j) w -> p j w", j=PACK)
            cols = slice(0, T) if h is None else slice(h * HALF, (h + 1) * HALF)
            nc.sync.dma_start(out=raw[k][:, :, cols], in_=src[:, :, cols])

        def load_w4(a):
            nc.sync.dma_start(out=w4[a][:].bitcast(I32), in_=w4_words[a].bitcast(I32))

        def convert(k):
            for h in range(2):
                c0, c1, c2 = h * HALF, h * HALF + V_COLS, (h + 1) * HALF
                nc.vector.tensor_copy(out=grouped[k][:, c0:c1, :], in_=raw[k][:, :, c0:c1].rearrange("p j w -> p w j"))
                nc.scalar.copy(out=grouped[k][:, c1:c2, :], in_=raw[k][:, :, c1:c2].rearrange("p j w -> p w j"))

        def quantize(k):
            for h in range(2):
                cols = slice(h * HALF, (h + 1) * HALF)
                nc.vector.quantize_mx(
                    out=codes[k][:, cols].bitcast(FP8X4),
                    scales=xscales[k][:, cols],
                    in_=grouped[k][:, cols, :].rearrange("p w j -> p (w j)"),
                )

        with tc.manual_schedule():
            nc.vector.memset(b_rows[:], 0.0)
            nc.vector.memset(s8[:].bitcast(I32), 0)
            nc.vector.memset(s4[:].bitcast(I32), 0)
            nc.vector.memset(warm[:], 0.0)
            make_identity(nc, ident[:])

            load_x(0)
            nc.sync.dma_start(out=w8[:].bitcast(I32), in_=w8_words[0].rearrange("p n t -> p (n t)").bitcast(I32))
            nc.scalar.dma_start(out=b_rows[0:N_M, :], in_=b.rearrange("(c p) -> c p", p=P))
            s8_src = w8_scales[0].bitcast(I32).rearrange("(q r) n -> r q n", r=4)
            for r in range(4):
                nc.scalar.dma_start(out=s8[:].bitcast(I32)[r:P:32, :], in_=s8_src[r])
            load_x(1)
            s4_src = w4_scales.bitcast(I32).rearrange("a (q r) n -> r q a n", r=4)
            s4_dst = s4[:].bitcast(I32).rearrange("p (a n) -> p a n", a=N_K - 1)
            for r in range(4):
                nc.scalar.dma_start(out=s4_dst[r:P:32, :, :], in_=s4_src[r])
            load_w4(0)
            load_x(2)
            load_w4(1)
            load_x(3)
            load_w4(2)
            load_x(4)
            load_x(5, 0)
            load_x(5, 1)
            load_w4(3)
            load_w4(4)

            nc.scalar.activation(out=warm[:], in_=warm[:], func=GELU)

            b_psum = psum.tile([P, T], F32, name="b_psum", tag="bank7")
            nc.tensor.transpose(b_psum[:, 0:P], b_rows[:], ident[:])
            nc.vector.tensor_copy(out=b_cols[:], in_=b_psum[:, 0:N_M])

            acc = [psum.tile([P, T], F32, name="acc%d" % m, tag="bank%d" % m) for m in range(N_M)]

            def multiply(k, m):
                cols = slice(m * P, (m + 1) * P)
                if k == 0:
                    lhsT = w8[:, cols].bitcast(FP8X4)
                    lhsT_scale = s8[:, cols]
                else:
                    lhsT = w4[k - 1][:, 2 * m * P : 2 * (m + 1) * P].bitcast(FP4X4)
                    lhsT_scale = s4[:, (k - 1) * M + m * P : (k - 1) * M + (m + 1) * P]
                nc.tensor.matmul_mx(
                    out=acc[m][:],
                    lhsT=lhsT,
                    lhsT_scale=lhsT_scale,
                    rhs=codes[k][:].bitcast(FP8X4),
                    rhs_scale=xscales[k][:],
                    start=(k == 0),
                    stop=(k == N_K - 1),
                )

            def finish(m, parts):
                width = T // parts
                for i in range(parts):
                    cols = slice(i * width, (i + 1) * width)
                    nc.scalar.activation(out=result[m][:, cols], in_=acc[m][:, cols], func=GELU, bias=b_cols[:, m : m + 1])
                    nc.sync.dma_start(out=out[m * P : (m + 1) * P, cols], in_=result[m][:, cols])

            for k in range(N_K - 2):
                convert(k)
                quantize(k)
                for m in range(N_M):
                    multiply(k, m)
            convert(4)
            quantize(4)
            convert(5)
            quantize(5)
            AHEAD = 4
            for m in range(AHEAD):
                multiply(4, m)
            for m in range(N_M):
                multiply(5, m)
                if m + AHEAD < N_M:
                    multiply(4, m + AHEAD)
                finish(m, 2 if m == N_M - 1 else 1)
